import numpy as np
import ml_dtypes


def mxq(x, axis, fmt="e4m3"):
    dtype, down = {"e4m3": (ml_dtypes.float8_e4m3fn, 7), "e5m2": (ml_dtypes.float8_e5m2, 14)}[fmt]
    v = np.moveaxis(np.asarray(x, np.float32).astype(ml_dtypes.bfloat16).astype(np.float64), axis, -1)
    blocks = v.reshape(v.shape[:-1] + (-1, 32))
    amax = np.abs(blocks).max(-1, keepdims=True)
    byte = np.maximum(np.where(amax > 0, np.frexp(amax)[1] - 1 + 127, 0) - down, 1)
    scale = np.exp2(byte - 127.0)
    codes = (blocks / scale).astype(np.float32).astype(dtype).astype(np.float64)
    return np.moveaxis((codes * scale).reshape(v.shape), -1, axis)


WIDE = False


def mx_kscale(k):
    if not WIDE:
        return np.ones(k)
    levels = np.array([10, -10, 5, -5, 0])
    if k % 512:
        return np.exp2(np.random.permutation(np.resize(levels, k // 32))).repeat(32)
    a = np.empty((k // 512, 16))
    for p in range(k // 512):
        a[p, :8] = np.random.permutation(np.resize(levels, 8))
        for g in range(8):
            far = levels[np.abs(levels - a[p, g]) >= 10]
            a[p, g + 8] = far[np.random.randint(len(far))]
    return np.exp2(a.ravel()).repeat(32)


def f64(x):
    return np.asarray(x).astype(np.float64)


def striped(idx):
    return np.tile(idx.reshape(-1, 16).T, (8, 1)).astype(np.uint16)


def unstriped(offs):
    return offs[:16].T.reshape(-1).astype(np.int64)


E2M1 = np.array([0.0, 0.5, 1.0, 1.5, 2.0, 3.0, 4.0, 6.0, -0.0, -0.5, -1.0, -1.5, -2.0, -3.0, -4.0, -6.0])


def pack_weight(w, fmt):
    k, n = w.shape
    w = f64(np.asarray(w, np.float32).astype(ml_dtypes.bfloat16)).reshape(k // 32, 32, n)
    amax = np.abs(w).max(1)
    if fmt == "e4m3":
        byte = np.frexp(amax)[1] - 1 + 127 - 7
    else:
        mant, ex = np.frexp(amax / 6.0)
        byte = np.where(mant > 0.5, ex, ex - 1) + 127
    byte = np.clip(np.where(amax > 0, byte, 1), 1, 254)
    scaled = (w * np.exp2(127.0 - byte)[:, None, :]).reshape(k, n).astype(np.float32)
    by_word = np.ascontiguousarray(scaled.reshape(k // 512, 128, 4, n).transpose(0, 1, 3, 2))
    if fmt == "e4m3":
        words = by_word.astype(ml_dtypes.float8_e4m3fn).view(np.uint8)
    else:
        c = by_word.astype(ml_dtypes.float4_e2m1fn).view(np.uint8) & 0xF
        words = (c[..., 0::2] | (c[..., 1::2] << 4)).reshape(k // 512, 128, 2 * n)
    return np.ascontiguousarray(words), np.ascontiguousarray(byte.astype(np.uint8).reshape(k // 512, 16, n))


def unpack_weight(words, scales, fmt):
    g, _, n = scales.shape
    words = np.ascontiguousarray(words).reshape(g, 128, n, -1)
    if fmt == "e4m3":
        vals = words.view(ml_dtypes.float8_e4m3fn).astype(np.float64)
    else:
        nib = np.empty((g, 128, n, 4), np.uint8)
        nib[..., 0::2] = words & 0xF
        nib[..., 1::2] = words >> 4
        vals = E2M1[nib]
    vals = vals * np.repeat(np.exp2(scales.astype(np.float64) - 127.0), 8, axis=1)[..., None]
    return vals.transpose(0, 1, 3, 2).reshape(g * 512, n)


def gelu(v):
    return 0.5 * v * (1.0 + np.tanh(np.sqrt(2.0 / np.pi) * (v + 0.044715 * v**3)))


K, T, S, H, T2, P = 1536, 2048, 512, 1024, 1024, 512

def setup_inputs():
    n = np.random.standard_normal
    s = mx_kscale(K)[:, None]
    u = mx_kscale(H)[:, None]
    d = {}
    d["tab_words"], d["tab_scales"] = pack_weight(n((K, T)) * s, "e4m3")
    d["offs"] = striped(np.random.permutation(T)[:S])
    d["w1_words"], d["w1_scales"] = pack_weight(2.5 * n((K, H)) / K**0.5 / s, "e2m1")
    d["gain"] = (1.3 * n(H) * u[:, 0]).astype(np.float32)
    d["page0"] = (n((H, T2)) * u).astype(np.float32)
    d["wgs"] = np.exp(0.3 * n((128, S))).astype(np.float32)
    d["offs2"] = striped(np.random.permutation(T2)[:S])
    d["offs3"] = striped(np.random.permutation(T2)[:P])
    d["vec"] = (n(H) / H**0.5 / u[:, 0]**2).astype(np.float32)
    d["query"] = (n((H, P)) / H**0.5 / u).astype(np.float32)
    d["base"] = (0.7 * n((T2, P))).astype(np.float32)
    return d

def reference(tab_words, tab_scales, offs, w1_words, w1_scales, gain, page0, wgs, offs2, offs3, vec, query, base):
    v = unpack_weight(tab_words, tab_scales, "e4m3")[:, unstriped(offs)]
    w1 = unpack_weight(w1_words, w1_scales, "e2m1")
    z = w1.T @ v
    h = f64(gain)[:, None] / (1.0 + np.exp(-z))
    page = f64(page0).copy()
    page[:, unstriped(offs2)] = np.tile(f64(wgs), (H // 128, 1)) * h
    x = np.abs(page[:, unstriped(offs3)]) * f64(vec)[:, None]
    pq = mxq(page, 0, "e4m3")
    e = pq.T @ mxq(x, 0, "e4m3")
    f = pq.T @ mxq(f64(query), 0, "e4m3")
    return np.maximum(e, f) + f64(base)

@@ -1,0 +1,294 @@
+from contextlib import ExitStack
+
+import concourse.mybir as mybir
+from concourse.masks import make_identity
+
+K, T, S, H, T2, NQ = 1536, 2048, 512, 1024, 1024, 512
+FLOPS = 2 * K * H * S + 2 * 2 * H * T2 * NQ
+
+F32 = mybir.dt.float32
+BF16 = mybir.dt.bfloat16
+I32 = mybir.dt.int32
+U32 = mybir.dt.uint32
+U16 = mybir.dt.uint16
+U8 = mybir.dt.uint8
+FP8X4 = mybir.dt.float8_e4m3fn_x4
+FP4X4 = mybir.dt.float4_e2m1fn_x4
+ACT = mybir.ActivationFunctionType
+ALU = mybir.AluOpType
+
+P = 128
+PACK = 4
+KP = K // (P * PACK)
+RP = H // (P * PACK)
+HALF = T2 // 2
+
+
+def tile_list_runway_alarm_match_kernel(
+    tc, tab_words, tab_scales, offs, w1_words, w1_scales, gain, page0, wgs, offs2, offs3, vec, query, base, out
+):
+    nc = tc.nc
+    with ExitStack() as ctx:
+        lists = ctx.enter_context(tc.tile_pool(name="lists", bufs=1))
+        keep = ctx.enter_context(tc.tile_pool(name="keep", bufs=1))
+        big = ctx.enter_context(tc.tile_pool(name="big", bufs=4))
+        ring = ctx.enter_context(tc.tile_pool(name="ring", bufs=8))
+        small = ctx.enter_context(tc.tile_pool(name="small", bufs=3))
+        psum = ctx.enter_context(tc.psum_pool(name="psum", bufs=8))
+
+        pick = lists.tile([P, S // 16], U16, name="pick")
+        place = lists.tile([P, S // 16], U16, name="place")
+        alarm = lists.tile([P, NQ // 16], U16, name="alarm")
+
+        tab_sc = keep.tile([P, KP, T], U8, name="tab_sc", align_bytes=64)
+        w1_sc_raw = keep.tile([P, KP, H], U8, name="w1_sc_raw", align_bytes=64)
+        tab_sc_words = tab_sc[:].rearrange("p a t -> p (a t)").bitcast(I32)
+        split = T // 4
+        nc.gpsimd.memset(tab_sc_words[:, 0:split], 0)
+        nc.vector.memset(tab_sc_words[:, split:], 0)
+        nc.vector.memset(w1_sc_raw[:].bitcast(I32), 0)
+        identity = keep.tile([P, P], F32, name="identity")
+        make_identity(nc, identity[:])
+
+        def load_tab(a):
+            t = big.tile([P, T], I32, name="tab%d" % a, tag="big")
+            words = tab_words[a].rearrange("p t i -> p (t i)").bitcast(I32)
+            for h in range(2):
+                cols = slice(h * T // 2, (h + 1) * T // 2)
+                nc.sync.dma_start(out=t[:, cols], in_=words[:, cols])
+            return t
+
+        def load_w1(b, pieces):
+            t = keep.tile([P, KP, 2 * P * PACK], U8, name="w1_raw%d" % b, align_bytes=64)
+            cols = slice(2 * P * PACK * b, 2 * P * PACK * (b + 1))
+            src = w1_words[:, :, cols].rearrange("a p n -> p a n")
+            for passes in pieces:
+                nc.sync.dma_start(out=t[:, passes, :].bitcast(I32), in_=src[:, passes, :].bitcast(I32))
+            return t
+
+        page_rows = page0.rearrange("(b p i) m -> b i p m", b=RP, i=PACK)
+
+        def load_page(b, i):
+            t = keep.tile([P, T2], F32, name="page%d%d" % (b, i))
+            nc.sync.dma_start(out=t[:], in_=page_rows[b, i])
+            return t
+
+        def load_rows(src, name):
+            t = big.tile([P, PACK, NQ], F32, name=name, tag="big")
+            nc.sync.dma_start(out=t[:], in_=src)
+            return t
+
+        nc.sync.dma_start(pick[:], offs)
+        for q in range(4):
+            nc.sync.dma_start(
+                out=tab_sc[32 * q : 32 * q + 4, :, :].bitcast(I32),
+                in_=tab_scales[:, 4 * q : 4 * q + 4, :].rearrange("a r t -> r a t").bitcast(I32),
+            )
+        tab = [load_tab(0)]
+        gain_t = keep.tile([P, RP, PACK], F32, name="gain_t")
+        vec_t = keep.tile([P, RP, PACK], F32, name="vec_t")
+        wg_raw = keep.tile([P, S], F32, name="wg_raw")
+        nc.sync.dma_start(out=wg_raw[:], in_=wgs)
+        nc.sync.dma_start(out=gain_t[:], in_=gain.rearrange("(b p i) -> p b i", b=RP, i=PACK))
+        nc.sync.dma_start(place[:], offs2)
+        nc.sync.dma_start(alarm[:], offs3)
+        nc.sync.dma_start(out=vec_t[:], in_=vec.rearrange("(b p i) -> p b i", b=RP, i=PACK))
+        w1_raw = [load_w1(0, [slice(a, a + 1) for a in range(KP)])]
+        tab.append(load_tab(1))
+        for q in range(4):
+            nc.sync.dma_start(
+                out=w1_sc_raw[32 * q : 32 * q + 4, :, :].bitcast(I32),
+                in_=w1_scales[:, 4 * q : 4 * q + 4, :].rearrange("a r c -> r a c").bitcast(I32),
+            )
+        tab.append(load_tab(2))
+        page = {(0, 0): load_page(0, 0)}
+        w1_raw.append(load_w1(1, [slice(0, KP)]))
+        page[0, 1] = load_page(0, 1)
+        query_rows = query.rearrange("(b p i) j -> b p i j", b=RP, i=PACK)
+        q_raw = [load_rows(query_rows[0], "q_raw0")]
+        page[0, 2] = load_page(0, 2)
+        q_raw.append(load_rows(query_rows[1], "q_raw1"))
+        page[0, 3] = load_page(0, 3)
+        for i in range(PACK):
+            page[1, i] = load_page(1, i)
+        base_rows = base.rearrange("(g n p) j -> g p n j", n=4, p=P)
+        base_t = [load_rows(base_rows[g], "base%d" % g) for g in range(2)]
+
+        v_words, v_scales = [], []
+
+        def gather_words(a, pieces):
+            vw = keep.tile([P, S], U32, name="v_words%d" % a, align_bytes=64)
+            n = S // pieces
+            for k in range(pieces):
+                window = tab[a][:].bitcast(U32).indirect(pick[:, k * n // 16 : (k + 1) * n // 16])
+                nc.vector.tensor_copy(out=vw[:, k * n : (k + 1) * n], in_=window)
+            v_words.append(vw)
+
+        gather_words(0, 1)
+        for a in range(KP):
+            vs = keep.tile([P, S], U8, name="v_scales%d" % a, align_bytes=64)
+            nc.vector.tensor_copy(out=vs[:], in_=tab_sc[:, a, :].indirect(pick[:]))
+            v_scales.append(vs)
+        gather_words(1, 1)
+        gather_words(2, 2)
+
+        turned = psum.tile([P, S // P, P], F32, name="turned", tag="bank")
+        for jb in range(S // P):
+            nc.tensor.transpose(turned[:, jb, :], wg_raw[:, P * jb : P * (jb + 1)], identity[:])
+        wg_dealt, feats = [], {}
+        for i in range(PACK):
+            spread = ring.tile([P, S // P, 4, 32], F32, name="spread", tag="ring_b", bufs=7)
+            src = turned[:].rearrange("j g (o p i) -> j g o p i", o=1, i=PACK)[:, :, :, :, i]
+            nc.scalar.copy(out=spread[:], in_=src.to_broadcast([P, S // P, 4, 32]))
+            back = psum.tile([P, S], F32, name="back", tag="bank")
+            for jb in range(S // P):
+                nc.tensor.transpose(
+                    back[:, P * jb : P * (jb + 1)], spread[:, jb, :, :].rearrange("j o p -> j (o p)"), identity[:]
+                )
+            wg = ring.tile([P, S], F32, name="wg", tag="ring_a")
+            nc.scalar.copy(out=wg[:], in_=back[:])
+            wg_dealt.append(wg)
+
+        def products(b):
+            banks = [psum.tile([P, P * PACK], F32, name="z%d" % jb, tag="bank") for jb in range(S // P)]
+            for a in range(KP):
+                for jb in range(S // P):
+                    cols = slice(P * jb, P * (jb + 1))
+                    nc.tensor.matmul_mx(
+                        out=banks[jb][:],
+                        lhsT=v_words[a][:, cols].bitcast(FP8X4),
+                        lhsT_scale=v_scales[a][:, cols],
+                        rhs=w1_raw[b][:, a, :].bitcast(FP4X4),
+                        rhs_scale=w1_sc_raw[:, a, P * PACK * b : P * PACK * (b + 1)],
+                        start=(a == 0),
+                        stop=(a == KP - 1),
+                    )
+            return banks
+
+        def sigmoids(sig, banks, blocks, rows):
+            for jb in blocks:
+                src = banks[jb][:].rearrange("j (p i) -> j i p", i=PACK)
+                nc.scalar.activation(out=sig[:, jb, rows, :], in_=src[:, rows, :], func=ACT.Sigmoid)
+
+        def feature_tile(b, i):
+            if (b, i) == (1, 2):
+                h = keep.tile([P, S], F32, name="h", tag="held", align_bytes=64)
+            else:
+                h = ring.tile([P, S], F32, name="h", tag="ring_b", bufs=7)
+            feats[b, i] = h
+
+        def turn_back(sig, b, i, blocks):
+            bank = psum.tile([P, P * len(blocks)], F32, name="h_bank", tag="bank")
+            for n, jb in enumerate(blocks):
+                nc.tensor.transpose(bank[:, P * n : P * (n + 1)], sig[:, jb, i, :], identity[:])
+            cols = slice(P * blocks[0], P * (blocks[-1] + 1))
+            nc.scalar.activation(out=feats[b, i][:, cols], in_=bank[:], func=ACT.Copy, scale=gain_t[:, b, i : i + 1])
+
+        for b in range(RP):
+            banks = products(b)
+            sig = keep.tile([P, S // P, PACK, P], F32, name="sig", tag="sig")
+            first = 1 if b == 0 else 0
+            if b == 0:
+                feature_tile(0, 0)
+                for blocks in ([0, 1], [2, 3]):
+                    sigmoids(sig, banks, blocks, slice(0, 1))
+                    turn_back(sig, 0, 0, blocks)
+            sigmoids(sig, banks, range(S // P), slice(first, PACK))
+            for i in range(first, PACK):
+                feature_tile(b, i)
+                turn_back(sig, b, i, [0, 1, 2, 3])
+
+        def weave(dst, src):
+            nc.scalar.copy(
+                out=dst.rearrange("p (c k) i -> p c i k", k=4), in_=src.rearrange("p i (c k) -> p c i k", k=4)
+            )
+
+        def quantise(src, name, scales=None):
+            width = src.shape[1]
+            codes = keep.tile([P, width], U32, name=name + "_codes", align_bytes=64)
+            if scales is None:
+                plane = keep.tile([P, width], U8, name=name + "_scales", align_bytes=64)
+                scales = plane[:]
+            nc.vector.quantize_mx(out=codes[:].bitcast(FP8X4), scales=scales, in_=src.rearrange("p c i -> p (c i)"))
+            return codes[:], scales
+
+        order = [(b, i) for b in range(RP) for i in range(PACK)]
+        pairs = [(0, 0), (0, 2), (1, 0)]
+        page_side = {k: keep.tile([P, 2, T2], F32, name="page_side%d%d" % k) for k in pairs}
+        x_side = {k: keep.tile([P, 2, NQ], BF16, name="x_side%d%d" % k) for k in pairs}
+        page_w = {
+            (b, h): keep.tile([P, HALF, PACK], BF16, name="page_w%d%d" % (b, h), align_bytes=64)
+            for b in range(RP)
+            for h in range(2)
+        }
+        x_w = [keep.tile([P, NQ, PACK], BF16, name="x_w%d" % b, align_bytes=64) for b in range(RP)]
+        q_w = [keep.tile([P, NQ, PACK], BF16, name="q_w%d" % b, align_bytes=64) for b in range(RP)]
+        page_q, x_q, q_q = {}, {}, {}
+
+        for b, i in order:
+            rows = page[b, i]
+            pieces = 2 if (b, i) == (0, 0) else 1
+            n = S // pieces
+            for k in range(pieces):
+                cols = slice(k * n, (k + 1) * n)
+                window = rows[:].indirect(place[:, k * n // 16 : (k + 1) * n // 16])
+                nc.vector.tensor_tensor(out=window, in0=feats[b, i][:, cols], in1=wg_dealt[i][:, cols], op=ALU.mult)
+            picked = small.tile([P, NQ], F32, name="picked", bufs=8)
+            nc.vector.tensor_copy(out=picked[:], in_=rows[:].indirect(alarm[:]))
+            scale = vec_t[:, b, i : i + 1]
+            size = small.tile([P, NQ], F32, name="size", bufs=2)
+            pair = (b, i - i % 2)
+            if pair in pairs:
+                queue = nc.gpsimd if pair == (0, 0) else nc.sync
+                queue.dma_start(out=page_side[pair][:, i % 2, :], in_=rows[:])
+                nc.scalar.activation(out=size[:], in_=picked[:], func=ACT.Abs)
+                nc.scalar.activation(out=x_side[pair][:, i % 2, :], in_=size[:], func=ACT.Copy, scale=scale)
+                if i % 2 == 1:
+                    weave(x_w[b][:, :, i - 1 : i + 1], x_side[pair][:])
+                    for h in range(2):
+                        weave(page_w[b, h][:, :, i - 1 : i + 1], page_side[pair][:, :, HALF * h : HALF * (h + 1)])
+            else:
+                nc.scalar.copy(out=page_w[b, 0][:, :, i], in_=rows[:, 0:HALF])
+                nc.scalar.activation(out=size[:], in_=picked[:], func=ACT.Abs)
+                nc.vector.tensor_copy(out=page_w[b, 1][:, :, i], in_=rows[:, HALF:T2])
+                nc.vector.tensor_scalar(
+                    out=x_w[b][:, :, i], in0=size[:], scalar1=scale, scalar2=None, op0=ALU.mult
+                )
+            if b == 0 and i in (1, 2):
+                weave(q_w[i - 1][:], q_raw[i - 1][:])
+            if (b, i) == (1, 2):
+                planes = keep.tile([P, 5, HALF], U8, name="planes", tag="held", align_bytes=64)
+                page_q[0, 0] = quantise(page_w[0, 0][:], "page00", planes[:, 0, :])
+                q_q[0] = quantise(q_w[0][:], "q0", planes[:, 1, :])
+                x_q[0] = quantise(x_w[0][:], "x0", planes[:, 2, :])
+                page_q[0, 1] = quantise(page_w[0, 1][:], "page01", planes[:, 3, :])
+                q_q[1] = quantise(q_w[1][:], "q1", planes[:, 4, :])
+        page_q[1, 0] = quantise(page_w[1, 0][:], "page10")
+        x_q[1] = quantise(x_w[1][:], "x1")
+        page_q[1, 1] = quantise(page_w[1, 1][:], "page11")
+
+        def scores(mt, moving):
+            acc = psum.tile([P, NQ], F32, name="acc", tag="bank")
+            h, cols = mt // 4, slice(P * (mt % 4), P * (mt % 4 + 1))
+            for b in range(RP):
+                nc.tensor.matmul_mx(
+                    out=acc[:],
+                    lhsT=page_q[b, h][0][:, cols].bitcast(FP8X4),
+                    lhsT_scale=page_q[b, h][1][:, cols],
+                    rhs=moving[b][0].bitcast(FP8X4),
+                    rhs_scale=moving[b][1],
+                    start=(b == 0),
+                    stop=(b == RP - 1),
+                )
+            return acc
+
+        for mt in range(T2 // P):
+            f = scores(mt, q_q)
+            e = scores(mt, x_q)
+            f_sb = ring.tile([P, NQ], F32, name="f_sb", tag="ring_a")
+            nc.scalar.copy(out=f_sb[:], in_=f[:])
+            larger = small.tile([P, NQ], F32, name="larger", tag="picked", bufs=8)
+            nc.vector.tensor_tensor(out=larger[:], in0=e[:], in1=f_sb[:], op=ALU.max)
+            result = ring.tile([P, NQ], F32, name="result", tag="ring_b", bufs=7)
+            nc.vector.tensor_tensor(out=result[:], in0=larger[:], in1=base_t[mt // 4][:, mt % 4, :], op=ALU.add)
+            nc.sync.dma_start(out=out[P * mt : P * (mt + 1), :], in_=result[:])

@@ -22,6 +22,8 @@ PACK = 4
 KP = K // (P * PACK)
 RP = H // (P * PACK)
 HALF = T2 // 2
+FIRST_PIECES = [[0, 1], [2, 3]]
+TAB_PLACE = [0, 8 * T, 4 * T]
 
 
 def tile_list_runway_alarm_match_kernel(
@@ -31,6 +33,7 @@ def tile_list_runway_alarm_match_kernel(
     with ExitStack() as ctx:
         lists = ctx.enter_context(tc.tile_pool(name="lists", bufs=1))
         keep = ctx.enter_context(tc.tile_pool(name="keep", bufs=1))
+        overlay = ctx.enter_context(tc.tile_pool(name="overlay", bufs=1))
         big = ctx.enter_context(tc.tile_pool(name="big", bufs=4))
         ring = ctx.enter_context(tc.tile_pool(name="ring", bufs=8))
         small = ctx.enter_context(tc.tile_pool(name="small", bufs=3))
@@ -50,26 +53,26 @@ def tile_list_runway_alarm_match_kernel(
         identity = keep.tile([P, P], F32, name="identity")
         make_identity(nc, identity[:])
 
-        def load_tab(a):
-            t = big.tile([P, T], I32, name="tab%d" % a, tag="big")
-            words = tab_words[a].rearrange("p t i -> p (t i)").bitcast(I32)
-            for h in range(2):
-                cols = slice(h * T // 2, (h + 1) * T // 2)
-                nc.sync.dma_start(out=t[:, cols], in_=words[:, cols])
-            return t
+        tab = [overlay.tile([P, T], I32, name="tab%d" % a, offset=TAB_PLACE[a]) for a in range(KP)]
 
-        def load_w1(b, pieces):
+        def load_tab(a, cols):
+            words = tab_words[a].rearrange("p t i -> p (t i)").bitcast(I32)
+            nc.sync.dma_start(out=tab[a][:, cols], in_=words[:, cols])
+
+        def load_w1(b):
             t = keep.tile([P, KP, 2 * P * PACK], U8, name="w1_raw%d" % b, align_bytes=64)
             cols = slice(2 * P * PACK * b, 2 * P * PACK * (b + 1))
             src = w1_words[:, :, cols].rearrange("a p n -> p a n")
-            for passes in pieces:
-                nc.sync.dma_start(out=t[:, passes, :].bitcast(I32), in_=src[:, passes, :].bitcast(I32))
+            nc.sync.dma_start(out=t[:].bitcast(I32), in_=src.bitcast(I32))
             return t
 
         page_rows = page0.rearrange("(b p i) m -> b i p m", b=RP, i=PACK)
 
         def load_page(b, i):
-            t = keep.tile([P, T2], F32, name="page%d%d" % (b, i))
+            if (b, i) == (1, 3):
+                t = overlay.tile([P, T2], F32, name="page%d%d" % (b, i), offset=0)
+            else:
+                t = keep.tile([P, T2], F32, name="page%d%d" % (b, i))
             nc.sync.dma_start(out=t[:], in_=page_rows[b, i])
             return t
 
@@ -84,37 +87,38 @@ def tile_list_runway_alarm_match_kernel(
                 out=tab_sc[32 * q : 32 * q + 4, :, :].bitcast(I32),
                 in_=tab_scales[:, 4 * q : 4 * q + 4, :].rearrange("a r t -> r a t").bitcast(I32),
             )
-        tab = [load_tab(0)]
+        load_tab(0, slice(0, T))
         gain_t = keep.tile([P, RP, PACK], F32, name="gain_t")
         vec_t = keep.tile([P, RP, PACK], F32, name="vec_t")
         wg_raw = keep.tile([P, S], F32, name="wg_raw")
         nc.sync.dma_start(out=wg_raw[:], in_=wgs)
-        nc.sync.dma_start(out=gain_t[:], in_=gain.rearrange("(b p i) -> p b i", b=RP, i=PACK))
-        nc.sync.dma_start(place[:], offs2)
-        nc.sync.dma_start(alarm[:], offs3)
-        nc.sync.dma_start(out=vec_t[:], in_=vec.rearrange("(b p i) -> p b i", b=RP, i=PACK))
-        w1_raw = [load_w1(0, [slice(a, a + 1) for a in range(KP)])]
-        tab.append(load_tab(1))
+        w1_raw = [load_w1(0)]
+        load_tab(1, slice(0, T // 2))
         for q in range(4):
             nc.sync.dma_start(
                 out=w1_sc_raw[32 * q : 32 * q + 4, :, :].bitcast(I32),
                 in_=w1_scales[:, 4 * q : 4 * q + 4, :].rearrange("a r c -> r a c").bitcast(I32),
             )
-        tab.append(load_tab(2))
+        load_tab(1, slice(T // 2, T))
+        load_tab(2, slice(0, T))
+        nc.sync.dma_start(out=gain_t[:], in_=gain.rearrange("(b p i) -> p b i", b=RP, i=PACK))
+        nc.sync.dma_start(place[:], offs2)
         page = {(0, 0): load_page(0, 0)}
-        w1_raw.append(load_w1(1, [slice(0, KP)]))
+        nc.sync.dma_start(alarm[:], offs3)
+        nc.sync.dma_start(out=vec_t[:], in_=vec.rearrange("(b p i) -> p b i", b=RP, i=PACK))
+        w1_raw.append(load_w1(1))
         page[0, 1] = load_page(0, 1)
         query_rows = query.rearrange("(b p i) j -> b p i j", b=RP, i=PACK)
         q_raw = [load_rows(query_rows[0], "q_raw0")]
         page[0, 2] = load_page(0, 2)
         q_raw.append(load_rows(query_rows[1], "q_raw1"))
         page[0, 3] = load_page(0, 3)
-        for i in range(PACK):
+        for i in range(PACK - 1):
             page[1, i] = load_page(1, i)
         base_rows = base.rearrange("(g n p) j -> g p n j", n=4, p=P)
         base_t = [load_rows(base_rows[g], "base%d" % g) for g in range(2)]
 
-        v_words, v_scales = [], []
+        v_words, v_scales = {}, {}
 
         def gather_words(a, pieces):
             vw = keep.tile([P, S], U32, name="v_words%d" % a, align_bytes=64)
@@ -122,13 +126,17 @@ def tile_list_runway_alarm_match_kernel(
             for k in range(pieces):
                 window = tab[a][:].bitcast(U32).indirect(pick[:, k * n // 16 : (k + 1) * n // 16])
                 nc.vector.tensor_copy(out=vw[:, k * n : (k + 1) * n], in_=window)
-            v_words.append(vw)
+            v_words[a] = vw
 
-        gather_words(0, 1)
-        for a in range(KP):
+        def gather_scales(a):
             vs = keep.tile([P, S], U8, name="v_scales%d" % a, align_bytes=64)
             nc.vector.tensor_copy(out=vs[:], in_=tab_sc[:, a, :].indirect(pick[:]))
-            v_scales.append(vs)
+            v_scales[a] = vs
+
+        gather_words(0, 1)
+        gather_scales(0)
+        gather_scales(1)
+        gather_scales(2)
         gather_words(1, 1)
         gather_words(2, 2)
 
@@ -171,8 +179,8 @@ def tile_list_runway_alarm_match_kernel(
                 nc.scalar.activation(out=sig[:, jb, rows, :], in_=src[:, rows, :], func=ACT.Sigmoid)
 
         def feature_tile(b, i):
-            if (b, i) == (1, 2):
-                h = keep.tile([P, S], F32, name="h", tag="held", align_bytes=64)
+            if b == 1 and i >= 2:
+                h = keep.tile([P, S], F32, name="h", tag="held%d" % i, align_bytes=64)
             else:
                 h = ring.tile([P, S], F32, name="h", tag="ring_b", bufs=7)
             feats[b, i] = h
@@ -190,7 +198,7 @@ def tile_list_runway_alarm_match_kernel(
             first = 1 if b == 0 else 0
             if b == 0:
                 feature_tile(0, 0)
-                for blocks in ([0, 1], [2, 3]):
+                for blocks in FIRST_PIECES:
                     sigmoids(sig, banks, blocks, slice(0, 1))
                     turn_back(sig, 0, 0, blocks)
             sigmoids(sig, banks, range(S // P), slice(first, PACK))
@@ -203,6 +211,9 @@ def tile_list_runway_alarm_match_kernel(
                 out=dst.rearrange("p (c k) i -> p c i k", k=4), in_=src.rearrange("p i (c k) -> p c i k", k=4)
             )
 
+        def weave_pair(dst, src):
+            nc.scalar.copy(out=dst, in_=src.rearrange("p i c -> p c i"))
+
         def quantise(src, name, scales=None):
             width = src.shape[1]
             codes = keep.tile([P, width], U32, name=name + "_codes", align_bytes=64)
@@ -213,57 +224,66 @@ def tile_list_runway_alarm_match_kernel(
             return codes[:], scales
 
         order = [(b, i) for b in range(RP) for i in range(PACK)]
-        pairs = [(0, 0), (0, 2), (1, 0)]
-        page_side = {k: keep.tile([P, 2, T2], F32, name="page_side%d%d" % k) for k in pairs}
-        x_side = {k: keep.tile([P, 2, NQ], BF16, name="x_side%d%d" % k) for k in pairs}
-        page_w = {
-            (b, h): keep.tile([P, HALF, PACK], BF16, name="page_w%d%d" % (b, h), align_bytes=64)
-            for b in range(RP)
-            for h in range(2)
-        }
+        copied = [PACK, 2]
+        page_side = [
+            overlay.tile([P, copied[b], T2], F32, name="page_side%d" % b, offset=4 * T2 * PACK * b) for b in range(RP)
+        ]
+        x_side = [keep.tile([P, copied[b], NQ], BF16, name="x_side%d" % b) for b in range(RP)]
+        page_w = {(0, h): keep.tile([P, HALF, PACK], BF16, name="page_w0%d" % h, align_bytes=64) for h in range(2)}
+        for h in range(2):
+            page_w[1, h] = overlay.tile(
+                [P, HALF, PACK], BF16, name="page_w1%d" % h, align_bytes=64, offset=8 * T2 + 8 * HALF * h
+            )
         x_w = [keep.tile([P, NQ, PACK], BF16, name="x_w%d" % b, align_bytes=64) for b in range(RP)]
         q_w = [keep.tile([P, NQ, PACK], BF16, name="q_w%d" % b, align_bytes=64) for b in range(RP)]
         page_q, x_q, q_q = {}, {}, {}
 
         for b, i in order:
             rows = page[b, i]
-            pieces = 2 if (b, i) == (0, 0) else 1
-            n = S // pieces
-            for k in range(pieces):
-                cols = slice(k * n, (k + 1) * n)
-                window = rows[:].indirect(place[:, k * n // 16 : (k + 1) * n // 16])
+            for blocks in FIRST_PIECES if (b, i) == (0, 0) else [[0, 1, 2, 3]]:
+                cols = slice(P * blocks[0], P * (blocks[-1] + 1))
+                window = rows[:].indirect(place[:, cols.start // 16 : cols.stop // 16])
                 nc.vector.tensor_tensor(out=window, in0=feats[b, i][:, cols], in1=wg_dealt[i][:, cols], op=ALU.mult)
             picked = small.tile([P, NQ], F32, name="picked", bufs=8)
             nc.vector.tensor_copy(out=picked[:], in_=rows[:].indirect(alarm[:]))
             scale = vec_t[:, b, i : i + 1]
-            size = small.tile([P, NQ], F32, name="size", bufs=2)
-            pair = (b, i - i % 2)
-            if pair in pairs:
-                queue = nc.gpsimd if pair == (0, 0) else nc.sync
-                queue.dma_start(out=page_side[pair][:, i % 2, :], in_=rows[:])
+            if b == 1 and i < 3:
+                size = overlay.tile([P, NQ], F32, name="size%d" % i, offset=4 * T2 + 4 * NQ * (i % 2))
+            else:
+                size = small.tile([P, NQ], F32, name="size", bufs=2)
+            if i < copied[b]:
+                nc.sync.dma_start(out=page_side[b][:, i, :], in_=rows[:])
                 nc.scalar.activation(out=size[:], in_=picked[:], func=ACT.Abs)
-                nc.scalar.activation(out=x_side[pair][:, i % 2, :], in_=size[:], func=ACT.Copy, scale=scale)
-                if i % 2 == 1:
-                    weave(x_w[b][:, :, i - 1 : i + 1], x_side[pair][:])
-                    for h in range(2):
-                        weave(page_w[b, h][:, :, i - 1 : i + 1], page_side[pair][:, :, HALF * h : HALF * (h + 1)])
+                nc.scalar.activation(out=x_side[b][:, i, :], in_=size[:], func=ACT.Copy, scale=scale)
+                if i == copied[b] - 1:
+                    join = weave if b == 0 else weave_pair
+                    join(x_w[b][:, :, 0 : i + 1], x_side[b][:])
+                    for h in range(2 - b):
+                        join(page_w[b, h][:, :, 0 : i + 1], page_side[b][:, :, HALF * h : HALF * (h + 1)])
+                    if b == 0:
+                        page[1, 3] = load_page(1, 3)
             else:
                 nc.scalar.copy(out=page_w[b, 0][:, :, i], in_=rows[:, 0:HALF])
                 nc.scalar.activation(out=size[:], in_=picked[:], func=ACT.Abs)
-                nc.vector.tensor_copy(out=page_w[b, 1][:, :, i], in_=rows[:, HALF:T2])
+                if i == 2:
+                    weave_pair(page_w[b, 1][:, :, 0:2], page_side[b][:, :, HALF:T2])
+                else:
+                    for r in (2, 3):
+                        nc.scalar.copy(out=page_w[b, 1][:, :, r], in_=page[b, r][:, HALF:T2])
                 nc.vector.tensor_scalar(
                     out=x_w[b][:, :, i], in0=size[:], scalar1=scale, scalar2=None, op0=ALU.mult
                 )
             if b == 0 and i in (1, 2):
                 weave(q_w[i - 1][:], q_raw[i - 1][:])
             if (b, i) == (1, 2):
-                planes = keep.tile([P, 5, HALF], U8, name="planes", tag="held", align_bytes=64)
+                planes = keep.tile([P, 3, HALF], U8, name="planes", tag="held2", align_bytes=64)
                 page_q[0, 0] = quantise(page_w[0, 0][:], "page00", planes[:, 0, :])
                 q_q[0] = quantise(q_w[0][:], "q0", planes[:, 1, :])
                 x_q[0] = quantise(x_w[0][:], "x0", planes[:, 2, :])
-                page_q[0, 1] = quantise(page_w[0, 1][:], "page01", planes[:, 3, :])
-                q_q[1] = quantise(q_w[1][:], "q1", planes[:, 4, :])
+        planes = keep.tile([P, 2, HALF], U8, name="late_planes", tag="held3", align_bytes=64)
+        q_q[1] = quantise(q_w[1][:], "q1", planes[:, 0, :])
         page_q[1, 0] = quantise(page_w[1, 0][:], "page10")
+        page_q[0, 1] = quantise(page_w[0, 1][:], "page01", planes[:, 1, :])
         x_q[1] = quantise(x_w[1][:], "x1")
         page_q[1, 1] = quantise(page_w[1, 1][:], "page11")
 

@@ -22,6 +22,7 @@ PACK = 4
 KP = K // (P * PACK)
 RP = H // (P * PACK)
 HALF = T2 // 2
+ADDS_ON_GPSIMD = 3
 FIRST_PIECES = [[0, 1], [2, 3]]
 TAB_PLACE = [0, 8 * T, 4 * T]
 
@@ -82,10 +83,10 @@ def tile_list_runway_alarm_match_kernel(
             return t
 
         nc.sync.dma_start(pick[:], offs)
-        for q in range(4):
+        for r in range(4):
             nc.sync.dma_start(
-                out=tab_sc[32 * q : 32 * q + 4, :, :].bitcast(I32),
-                in_=tab_scales[:, 4 * q : 4 * q + 4, :].rearrange("a r t -> r a t").bitcast(I32),
+                out=tab_sc[r:P:32, :, :].bitcast(I32),
+                in_=tab_scales.rearrange("a (q r) t -> r q a t", r=4)[r].bitcast(I32),
             )
         load_tab(0, slice(0, T))
         gain_t = keep.tile([P, RP, PACK], F32, name="gain_t")
@@ -94,10 +95,10 @@ def tile_list_runway_alarm_match_kernel(
         nc.sync.dma_start(out=wg_raw[:], in_=wgs)
         w1_raw = [load_w1(0)]
         load_tab(1, slice(0, T // 2))
-        for q in range(4):
+        for r in range(4):
             nc.sync.dma_start(
-                out=w1_sc_raw[32 * q : 32 * q + 4, :, :].bitcast(I32),
-                in_=w1_scales[:, 4 * q : 4 * q + 4, :].rearrange("a r c -> r a c").bitcast(I32),
+                out=w1_sc_raw[r:P:32, :, :].bitcast(I32),
+                in_=w1_scales.rearrange("a (q r) c -> r q a c", r=4)[r].bitcast(I32),
             )
         load_tab(1, slice(T // 2, T))
         load_tab(2, slice(0, T))
@@ -144,15 +145,17 @@ def tile_list_runway_alarm_match_kernel(
         for jb in range(S // P):
             nc.tensor.transpose(turned[:, jb, :], wg_raw[:, P * jb : P * (jb + 1)], identity[:])
         wg_dealt, feats = [], {}
+        spread = keep.tile([P, PACK, S // P, P], F32, name="spread")
+        for jb in range(S // P):
+            src = turned[:, jb : jb + 1, :].to_broadcast([P, 4, P])
+            nc.scalar.copy(
+                out=spread[:, :, jb, :].rearrange("j i (o c k) -> j o c i k", o=4, k=4),
+                in_=src.rearrange("j o (c k i) -> j o c i k", k=4, i=PACK),
+            )
         for i in range(PACK):
-            spread = ring.tile([P, S // P, 4, 32], F32, name="spread", tag="ring_b", bufs=7)
-            src = turned[:].rearrange("j g (o p i) -> j g o p i", o=1, i=PACK)[:, :, :, :, i]
-            nc.scalar.copy(out=spread[:], in_=src.to_broadcast([P, S // P, 4, 32]))
             back = psum.tile([P, S], F32, name="back", tag="bank")
             for jb in range(S // P):
-                nc.tensor.transpose(
-                    back[:, P * jb : P * (jb + 1)], spread[:, jb, :, :].rearrange("j o p -> j (o p)"), identity[:]
-                )
+                nc.tensor.transpose(back[:, P * jb : P * (jb + 1)], spread[:, i, jb, :], identity[:])
             wg = ring.tile([P, S], F32, name="wg", tag="ring_a")
             nc.scalar.copy(out=wg[:], in_=back[:])
             wg_dealt.append(wg)
@@ -175,8 +178,9 @@ def tile_list_runway_alarm_match_kernel(
 
         def sigmoids(sig, banks, blocks, rows):
             for jb in blocks:
-                src = banks[jb][:].rearrange("j (p i) -> j i p", i=PACK)
-                nc.scalar.activation(out=sig[:, jb, rows, :], in_=src[:, rows, :], func=ACT.Sigmoid)
+                src = banks[jb][:].rearrange("j (c k i) -> j c i k", k=4, i=PACK)
+                dst = sig[:, jb, :, :].rearrange("j i (c k) -> j c i k", k=4)
+                nc.scalar.activation(out=dst[:, :, rows, :], in_=src[:, :, rows, :], func=ACT.Sigmoid)
 
         def feature_tile(b, i):
             if b == 1 and i >= 2:
@@ -268,8 +272,7 @@ def tile_list_runway_alarm_match_kernel(
                 if i == 2:
                     weave_pair(page_w[b, 1][:, :, 0:2], page_side[b][:, :, HALF:T2])
                 else:
-                    for r in (2, 3):
-                        nc.scalar.copy(out=page_w[b, 1][:, :, r], in_=page[b, r][:, HALF:T2])
+                    nc.scalar.copy(out=page_w[b, 1][:, :, 2], in_=page[b, 2][:, HALF:T2])
                 nc.vector.tensor_scalar(
                     out=x_w[b][:, :, i], in0=size[:], scalar1=scale, scalar2=None, op0=ALU.mult
                 )
@@ -285,7 +288,6 @@ def tile_list_runway_alarm_match_kernel(
         page_q[1, 0] = quantise(page_w[1, 0][:], "page10")
         page_q[0, 1] = quantise(page_w[0, 1][:], "page01", planes[:, 1, :])
         x_q[1] = quantise(x_w[1][:], "x1")
-        page_q[1, 1] = quantise(page_w[1, 1][:], "page11")
 
         def scores(mt, moving):
             acc = psum.tile([P, NQ], F32, name="acc", tag="bank")
@@ -302,13 +304,26 @@ def tile_list_runway_alarm_match_kernel(
                 )
             return acc
 
-        for mt in range(T2 // P):
+        def query_scores(mt):
             f = scores(mt, q_q)
-            e = scores(mt, x_q)
             f_sb = ring.tile([P, NQ], F32, name="f_sb", tag="ring_a")
             nc.scalar.copy(out=f_sb[:], in_=f[:])
+            return f_sb
+
+        def finish(mt, f_sb):
+            e = scores(mt, x_q)
             larger = small.tile([P, NQ], F32, name="larger", tag="picked", bufs=8)
             nc.vector.tensor_tensor(out=larger[:], in0=e[:], in1=f_sb[:], op=ALU.max)
             result = ring.tile([P, NQ], F32, name="result", tag="ring_b", bufs=7)
-            nc.vector.tensor_tensor(out=result[:], in0=larger[:], in1=base_t[mt // 4][:, mt % 4, :], op=ALU.add)
+            adder = nc.gpsimd if mt < ADDS_ON_GPSIMD else nc.vector
+            adder.tensor_tensor(out=result[:], in0=larger[:], in1=base_t[mt // 4][:, mt % 4, :], op=ALU.add)
             nc.sync.dma_start(out=out[P * mt : P * (mt + 1), :], in_=result[:])
+
+        first_half = [query_scores(mt) for mt in range(4)]
+        nc.scalar.copy(out=page_w[1, 1][:, :, 3], in_=page[1, 3][:, HALF:T2])
+        for mt in range(4):
+            finish(mt, first_half[mt])
+            if mt == 1:
+                page_q[1, 1] = quantise(page_w[1, 1][:], "page11")
+        for mt in range(4, T2 // P):
+            finish(mt, query_scores(mt))

@@ -183,8 +183,8 @@ def tile_list_runway_alarm_match_kernel(
                 nc.scalar.activation(out=dst[:, :, rows, :], in_=src[:, :, rows, :], func=ACT.Sigmoid)
 
         def feature_tile(b, i):
-            if b == 1 and i >= 2:
-                h = keep.tile([P, S], F32, name="h", tag="held%d" % i, align_bytes=64)
+            if i % 2 == 1 or (b, i) == (1, 2):
+                h = keep.tile([P, S], F32, name="h", tag="held%d%d" % (b, i), align_bytes=64)
             else:
                 h = ring.tile([P, S], F32, name="h", tag="ring_b", bufs=7)
             feats[b, i] = h
@@ -242,13 +242,24 @@ def tile_list_runway_alarm_match_kernel(
         q_w = [keep.tile([P, NQ, PACK], BF16, name="q_w%d" % b, align_bytes=64) for b in range(RP)]
         page_q, x_q, q_q = {}, {}, {}
 
-        for b, i in order:
-            rows = page[b, i]
+        def put(b, i):
             for blocks in FIRST_PIECES if (b, i) == (0, 0) else [[0, 1, 2, 3]]:
                 cols = slice(P * blocks[0], P * (blocks[-1] + 1))
-                window = rows[:].indirect(place[:, cols.start // 16 : cols.stop // 16])
+                window = page[b, i][:].indirect(place[:, cols.start // 16 : cols.stop // 16])
                 nc.vector.tensor_tensor(out=window, in0=feats[b, i][:, cols], in1=wg_dealt[i][:, cols], op=ALU.mult)
-            picked = small.tile([P, NQ], F32, name="picked", bufs=8)
+            if i < copied[b]:
+                nc.sync.dma_start(out=page_side[b][:, i, :], in_=page[b, i][:])
+
+        for b, i in order:
+            rows = page[b, i]
+            if i < copied[b] and i % 2 == 0:
+                put(b, i)
+                put(b, i + 1)
+                picked = keep.tile([P, NQ], F32, name="picked", tag="held%d%d" % (b, i + 1), align_bytes=64)
+            else:
+                if i >= copied[b]:
+                    put(b, i)
+                picked = small.tile([P, NQ], F32, name="picked", bufs=8)
             nc.vector.tensor_copy(out=picked[:], in_=rows[:].indirect(alarm[:]))
             scale = vec_t[:, b, i : i + 1]
             if b == 1 and i < 3:
@@ -256,7 +267,6 @@ def tile_list_runway_alarm_match_kernel(
             else:
                 size = small.tile([P, NQ], F32, name="size", bufs=2)
             if i < copied[b]:
-                nc.sync.dma_start(out=page_side[b][:, i, :], in_=rows[:])
                 nc.scalar.activation(out=size[:], in_=picked[:], func=ACT.Abs)
                 nc.scalar.activation(out=x_side[b][:, i, :], in_=size[:], func=ACT.Copy, scale=scale)
                 if i == copied[b] - 1:
@@ -272,22 +282,24 @@ def tile_list_runway_alarm_match_kernel(
                 if i == 2:
                     weave_pair(page_w[b, 1][:, :, 0:2], page_side[b][:, :, HALF:T2])
                 else:
-                    nc.scalar.copy(out=page_w[b, 1][:, :, 2], in_=page[b, 2][:, HALF:T2])
+                    for r in (2, 3):
+                        nc.scalar.copy(out=page_w[b, 1][:, :, r], in_=page[b, r][:, HALF:T2])
                 nc.vector.tensor_scalar(
                     out=x_w[b][:, :, i], in0=size[:], scalar1=scale, scalar2=None, op0=ALU.mult
                 )
             if b == 0 and i in (1, 2):
                 weave(q_w[i - 1][:], q_raw[i - 1][:])
             if (b, i) == (1, 2):
-                planes = keep.tile([P, 3, HALF], U8, name="planes", tag="held2", align_bytes=64)
+                planes = keep.tile([P, 3, HALF], U8, name="planes", tag="held12", align_bytes=64)
                 page_q[0, 0] = quantise(page_w[0, 0][:], "page00", planes[:, 0, :])
                 q_q[0] = quantise(q_w[0][:], "q0", planes[:, 1, :])
                 x_q[0] = quantise(x_w[0][:], "x0", planes[:, 2, :])
-        planes = keep.tile([P, 2, HALF], U8, name="late_planes", tag="held3", align_bytes=64)
+        planes = keep.tile([P, 2, HALF], U8, name="late_planes", tag="held13", align_bytes=64)
         q_q[1] = quantise(q_w[1][:], "q1", planes[:, 0, :])
         page_q[1, 0] = quantise(page_w[1, 0][:], "page10")
         page_q[0, 1] = quantise(page_w[0, 1][:], "page01", planes[:, 1, :])
         x_q[1] = quantise(x_w[1][:], "x1")
+        page_q[1, 1] = quantise(page_w[1, 1][:], "page11")
 
         def scores(mt, moving):
             acc = psum.tile([P, NQ], F32, name="acc", tag="bank")
@@ -320,10 +332,7 @@ def tile_list_runway_alarm_match_kernel(
             nc.sync.dma_start(out=out[P * mt : P * (mt + 1), :], in_=result[:])
 
         first_half = [query_scores(mt) for mt in range(4)]
-        nc.scalar.copy(out=page_w[1, 1][:, :, 3], in_=page[1, 3][:, HALF:T2])
         for mt in range(4):
             finish(mt, first_half[mt])
-            if mt == 1:
-                page_q[1, 1] = quantise(page_w[1, 1][:], "page11")
         for mt in range(4, T2 // P):
             finish(mt, query_scores(mt))

@@ -104,15 +104,15 @@ def tile_list_runway_alarm_match_kernel(
         load_tab(2, slice(0, T))
         nc.sync.dma_start(out=gain_t[:], in_=gain.rearrange("(b p i) -> p b i", b=RP, i=PACK))
         nc.sync.dma_start(place[:], offs2)
+        query_rows = query.rearrange("(b p i) j -> b p i j", b=RP, i=PACK)
+        q_raw = [load_rows(query_rows[0], "q_raw0")]
         page = {(0, 0): load_page(0, 0)}
         nc.sync.dma_start(alarm[:], offs3)
         nc.sync.dma_start(out=vec_t[:], in_=vec.rearrange("(b p i) -> p b i", b=RP, i=PACK))
         w1_raw.append(load_w1(1))
         page[0, 1] = load_page(0, 1)
-        query_rows = query.rearrange("(b p i) j -> b p i j", b=RP, i=PACK)
-        q_raw = [load_rows(query_rows[0], "q_raw0")]
-        page[0, 2] = load_page(0, 2)
         q_raw.append(load_rows(query_rows[1], "q_raw1"))
+        page[0, 2] = load_page(0, 2)
         page[0, 3] = load_page(0, 3)
         for i in range(PACK - 1):
             page[1, i] = load_page(1, i)
@@ -183,7 +183,7 @@ def tile_list_runway_alarm_match_kernel(
                 nc.scalar.activation(out=dst[:, :, rows, :], in_=src[:, :, rows, :], func=ACT.Sigmoid)
 
         def feature_tile(b, i):
-            if i % 2 == 1 or (b, i) == (1, 2):
+            if i == 1 or (b == 1 and i >= 2):
                 h = keep.tile([P, S], F32, name="h", tag="held%d%d" % (b, i), align_bytes=64)
             else:
                 h = ring.tile([P, S], F32, name="h", tag="ring_b", bufs=7)
@@ -242,6 +242,11 @@ def tile_list_runway_alarm_match_kernel(
         q_w = [keep.tile([P, NQ, PACK], BF16, name="q_w%d" % b, align_bytes=64) for b in range(RP)]
         page_q, x_q, q_q = {}, {}, {}
 
+        nc.vector.tensor_copy(
+            out=q_w[0][:].rearrange("p (c k) i -> p c i k", k=4), in_=q_raw[0][:].rearrange("p i (c k) -> p c i k", k=4)
+        )
+        q_q[0] = quantise(q_w[0][:], "q0")
+
         def put(b, i):
             for blocks in FIRST_PIECES if (b, i) == (0, 0) else [[0, 1, 2, 3]]:
                 cols = slice(P * blocks[0], P * (blocks[-1] + 1))
@@ -252,12 +257,12 @@ def tile_list_runway_alarm_match_kernel(
 
         for b, i in order:
             rows = page[b, i]
-            if i < copied[b] and i % 2 == 0:
+            if i == 0:
                 put(b, i)
                 put(b, i + 1)
                 picked = keep.tile([P, NQ], F32, name="picked", tag="held%d%d" % (b, i + 1), align_bytes=64)
             else:
-                if i >= copied[b]:
+                if i >= 2:
                     put(b, i)
                 picked = small.tile([P, NQ], F32, name="picked", bufs=8)
             nc.vector.tensor_copy(out=picked[:], in_=rows[:].indirect(alarm[:]))
@@ -287,13 +292,12 @@ def tile_list_runway_alarm_match_kernel(
                 nc.vector.tensor_scalar(
                     out=x_w[b][:, :, i], in0=size[:], scalar1=scale, scalar2=None, op0=ALU.mult
                 )
-            if b == 0 and i in (1, 2):
-                weave(q_w[i - 1][:], q_raw[i - 1][:])
+            if (b, i) == (0, 1):
+                weave(q_w[1][:], q_raw[1][:])
             if (b, i) == (1, 2):
-                planes = keep.tile([P, 3, HALF], U8, name="planes", tag="held12", align_bytes=64)
+                planes = keep.tile([P, 2, HALF], U8, name="planes", tag="held12", align_bytes=64)
                 page_q[0, 0] = quantise(page_w[0, 0][:], "page00", planes[:, 0, :])
-                q_q[0] = quantise(q_w[0][:], "q0", planes[:, 1, :])
-                x_q[0] = quantise(x_w[0][:], "x0", planes[:, 2, :])
+                x_q[0] = quantise(x_w[0][:], "x0", planes[:, 1, :])
         planes = keep.tile([P, 2, HALF], U8, name="late_planes", tag="held13", align_bytes=64)
         q_q[1] = quantise(q_w[1][:], "q1", planes[:, 0, :])
         page_q[1, 0] = quantise(page_w[1, 0][:], "page10")

from contextlib import ExitStack

import concourse.mybir as mybir
from concourse.masks import make_identity

K, T, S, H, T2, NQ = 1536, 2048, 512, 1024, 1024, 512
FLOPS = 2 * K * H * S + 2 * 2 * H * T2 * NQ

F32 = mybir.dt.float32
BF16 = mybir.dt.bfloat16
I32 = mybir.dt.int32
U32 = mybir.dt.uint32
U16 = mybir.dt.uint16
U8 = mybir.dt.uint8
FP8X4 = mybir.dt.float8_e4m3fn_x4
FP4X4 = mybir.dt.float4_e2m1fn_x4
ACT = mybir.ActivationFunctionType
ALU = mybir.AluOpType

P = 128
PACK = 4
KP = K // (P * PACK)
RP = H // (P * PACK)
HALF = T2 // 2
ADDS_ON_GPSIMD = 3
FIRST_PIECES = [[0, 1], [2, 3]]
TAB_PLACE = [0, 8 * T, 4 * T]


def tile_list_runway_alarm_match_kernel(
    tc, tab_words, tab_scales, offs, w1_words, w1_scales, gain, page0, wgs, offs2, offs3, vec, query, base, out
):
    nc = tc.nc
    with ExitStack() as ctx:
        lists = ctx.enter_context(tc.tile_pool(name="lists", bufs=1))
        keep = ctx.enter_context(tc.tile_pool(name="keep", bufs=1))
        overlay = ctx.enter_context(tc.tile_pool(name="overlay", bufs=1))
        big = ctx.enter_context(tc.tile_pool(name="big", bufs=4))
        ring = ctx.enter_context(tc.tile_pool(name="ring", bufs=8))
        small = ctx.enter_context(tc.tile_pool(name="small", bufs=3))
        psum = ctx.enter_context(tc.psum_pool(name="psum", bufs=8))

        pick = lists.tile([P, S // 16], U16, name="pick")
        place = lists.tile([P, S // 16], U16, name="place")
        alarm = lists.tile([P, NQ // 16], U16, name="alarm")

        tab_sc = keep.tile([P, KP, T], U8, name="tab_sc", align_bytes=64)
        w1_sc_raw = keep.tile([P, KP, H], U8, name="w1_sc_raw", align_bytes=64)
        tab_sc_words = tab_sc[:].rearrange("p a t -> p (a t)").bitcast(I32)
        split = T // 4
        nc.gpsimd.memset(tab_sc_words[:, 0:split], 0)
        nc.vector.memset(tab_sc_words[:, split:], 0)
        nc.vector.memset(w1_sc_raw[:].bitcast(I32), 0)
        identity = keep.tile([P, P], F32, name="identity")
        make_identity(nc, identity[:])

        tab = [overlay.tile([P, T], I32, name="tab%d" % a, offset=TAB_PLACE[a]) for a in range(KP)]

        def load_tab(a, cols):
            words = tab_words[a].rearrange("p t i -> p (t i)").bitcast(I32)
            nc.sync.dma_start(out=tab[a][:, cols], in_=words[:, cols])

        def load_w1(b):
            t = keep.tile([P, KP, 2 * P * PACK], U8, name="w1_raw%d" % b, align_bytes=64)
            cols = slice(2 * P * PACK * b, 2 * P * PACK * (b + 1))
            src = w1_words[:, :, cols].rearrange("a p n -> p a n")
            nc.sync.dma_start(out=t[:].bitcast(I32), in_=src.bitcast(I32))
            return t

        page_rows = page0.rearrange("(b p i) m -> b i p m", b=RP, i=PACK)

        def load_page(b, i):
            if (b, i) == (1, 3):
                t = overlay.tile([P, T2], F32, name="page%d%d" % (b, i), offset=0)
            else:
                t = keep.tile([P, T2], F32, name="page%d%d" % (b, i))
            nc.sync.dma_start(out=t[:], in_=page_rows[b, i])
            return t

        def load_rows(src, name):
            t = big.tile([P, PACK, NQ], F32, name=name, tag="big")
            nc.sync.dma_start(out=t[:], in_=src)
            return t

        nc.sync.dma_start(pick[:], offs)
        for r in range(4):
            nc.sync.dma_start(
                out=tab_sc[r:P:32, :, :].bitcast(I32),
                in_=tab_scales.rearrange("a (q r) t -> r q a t", r=4)[r].bitcast(I32),
            )
        load_tab(0, slice(0, T))
        gain_t = keep.tile([P, RP, PACK], F32, name="gain_t")
        vec_t = keep.tile([P, RP, PACK], F32, name="vec_t")
        wg_raw = keep.tile([P, S], F32, name="wg_raw")
        nc.sync.dma_start(out=wg_raw[:], in_=wgs)
        w1_raw = [load_w1(0)]
        load_tab(1, slice(0, T // 2))
        for r in range(4):
            nc.sync.dma_start(
                out=w1_sc_raw[r:P:32, :, :].bitcast(I32),
                in_=w1_scales.rearrange("a (q r) c -> r q a c", r=4)[r].bitcast(I32),
            )
        load_tab(1, slice(T // 2, T))
        load_tab(2, slice(0, T))
        nc.sync.dma_start(out=gain_t[:], in_=gain.rearrange("(b p i) -> p b i", b=RP, i=PACK))
        nc.sync.dma_start(place[:], offs2)
        query_rows = query.rearrange("(b p i) j -> b p i j", b=RP, i=PACK)
        q_raw = [load_rows(query_rows[0], "q_raw0")]
        page = {(0, 0): load_page(0, 0)}
        nc.sync.dma_start(alarm[:], offs3)
        nc.sync.dma_start(out=vec_t[:], in_=vec.rearrange("(b p i) -> p b i", b=RP, i=PACK))
        w1_raw.append(load_w1(1))
        page[0, 1] = load_page(0, 1)
        q_raw.append(load_rows(query_rows[1], "q_raw1"))
        page[0, 2] = load_page(0, 2)
        page[0, 3] = load_page(0, 3)
        for i in range(PACK - 1):
            page[1, i] = load_page(1, i)
        base_rows = base.rearrange("(g n p) j -> g p n j", n=4, p=P)
        base_t = [load_rows(base_rows[g], "base%d" % g) for g in range(2)]

        v_words, v_scales = {}, {}

        def gather_words(a, pieces):
            vw = keep.tile([P, S], U32, name="v_words%d" % a, align_bytes=64)
            n = S // pieces
            for k in range(pieces):
                window = tab[a][:].bitcast(U32).indirect(pick[:, k * n // 16 : (k + 1) * n // 16])
                nc.vector.tensor_copy(out=vw[:, k * n : (k + 1) * n], in_=window)
            v_words[a] = vw

        def gather_scales(a):
            vs = keep.tile([P, S], U8, name="v_scales%d" % a, align_bytes=64)
            nc.vector.tensor_copy(out=vs[:], in_=tab_sc[:, a, :].indirect(pick[:]))
            v_scales[a] = vs

        gather_words(0, 1)
        gather_scales(0)
        gather_scales(1)
        gather_scales(2)
        gather_words(1, 1)
        gather_words(2, 2)

        turned = psum.tile([P, S // P, P], F32, name="turned", tag="bank")
        for jb in range(S // P):
            nc.tensor.transpose(turned[:, jb, :], wg_raw[:, P * jb : P * (jb + 1)], identity[:])
        wg_dealt, feats = [], {}
        spread = keep.tile([P, PACK, S // P, P], F32, name="spread")
        for jb in range(S // P):
            src = turned[:, jb : jb + 1, :].to_broadcast([P, 4, P])
            nc.scalar.copy(
                out=spread[:, :, jb, :].rearrange("j i (o c k) -> j o c i k", o=4, k=4),
                in_=src.rearrange("j o (c k i) -> j o c i k", k=4, i=PACK),
            )
        for i in range(PACK):
            back = psum.tile([P, S], F32, name="back", tag="bank")
            for jb in range(S // P):
                nc.tensor.transpose(back[:, P * jb : P * (jb + 1)], spread[:, i, jb, :], identity[:])
            wg = ring.tile([P, S], F32, name="wg", tag="ring_a")
            nc.scalar.copy(out=wg[:], in_=back[:])
            wg_dealt.append(wg)

        def products(b):
            banks = [psum.tile([P, P * PACK], F32, name="z%d" % jb, tag="bank") for jb in range(S // P)]
            for a in range(KP):
                for jb in range(S // P):
                    cols = slice(P * jb, P * (jb + 1))
                    nc.tensor.matmul_mx(
                        out=banks[jb][:],
                        lhsT=v_words[a][:, cols].bitcast(FP8X4),
                        lhsT_scale=v_scales[a][:, cols],
                        rhs=w1_raw[b][:, a, :].bitcast(FP4X4),
                        rhs_scale=w1_sc_raw[:, a, P * PACK * b : P * PACK * (b + 1)],
                        start=(a == 0),
                        stop=(a == KP - 1),
                    )
            return banks

        def sigmoids(sig, banks, blocks, rows):
            for jb in blocks:
                src = banks[jb][:].rearrange("j (c k i) -> j c i k", k=4, i=PACK)
                dst = sig[:, jb, :, :].rearrange("j i (c k) -> j c i k", k=4)
                nc.scalar.activation(out=dst[:, :, rows, :], in_=src[:, :, rows, :], func=ACT.Sigmoid)

        def feature_tile(b, i):
            if i == 1 or (b == 1 and i >= 2):
                h = keep.tile([P, S], F32, name="h", tag="held%d%d" % (b, i), align_bytes=64)
            else:
                h = ring.tile([P, S], F32, name="h", tag="ring_b", bufs=7)
            feats[b, i] = h

        def turn_back(sig, b, i, blocks):
            bank = psum.tile([P, P * len(blocks)], F32, name="h_bank", tag="bank")
            for n, jb in enumerate(blocks):
                nc.tensor.transpose(bank[:, P * n : P * (n + 1)], sig[:, jb, i, :], identity[:])
            cols = slice(P * blocks[0], P * (blocks[-1] + 1))
            nc.scalar.activation(out=feats[b, i][:, cols], in_=bank[:], func=ACT.Copy, scale=gain_t[:, b, i : i + 1])

        for b in range(RP):
            banks = products(b)
            sig = keep.tile([P, S // P, PACK, P], F32, name="sig", tag="sig")
            first = 1 if b == 0 else 0
            if b == 0:
                feature_tile(0, 0)
                for blocks in FIRST_PIECES:
                    sigmoids(sig, banks, blocks, slice(0, 1))
                    turn_back(sig, 0, 0, blocks)
            sigmoids(sig, banks, range(S // P), slice(first, PACK))
            for i in range(first, PACK):
                feature_tile(b, i)
                turn_back(sig, b, i, [0, 1, 2, 3])

        def weave(dst, src):
            nc.scalar.copy(
                out=dst.rearrange("p (c k) i -> p c i k", k=4), in_=src.rearrange("p i (c k) -> p c i k", k=4)
            )

        def weave_pair(dst, src):
            nc.scalar.copy(out=dst, in_=src.rearrange("p i c -> p c i"))

        def quantise(src, name, scales=None):
            width = src.shape[1]
            codes = keep.tile([P, width], U32, name=name + "_codes", align_bytes=64)
            if scales is None:
                plane = keep.tile([P, width], U8, name=name + "_scales", align_bytes=64)
                scales = plane[:]
            nc.vector.quantize_mx(out=codes[:].bitcast(FP8X4), scales=scales, in_=src.rearrange("p c i -> p (c i)"))
            return codes[:], scales

        order = [(b, i) for b in range(RP) for i in range(PACK)]
        copied = [PACK, 2]
        page_side = [
            overlay.tile([P, copied[b], T2], F32, name="page_side%d" % b, offset=4 * T2 * PACK * b) for b in range(RP)
        ]
        x_side = [keep.tile([P, copied[b], NQ], BF16, name="x_side%d" % b) for b in range(RP)]
        page_w = {(0, h): keep.tile([P, HALF, PACK], BF16, name="page_w0%d" % h, align_bytes=64) for h in range(2)}
        for h in range(2):
            page_w[1, h] = overlay.tile(
                [P, HALF, PACK], BF16, name="page_w1%d" % h, align_bytes=64, offset=8 * T2 + 8 * HALF * h
            )
        x_w = [keep.tile([P, NQ, PACK], BF16, name="x_w%d" % b, align_bytes=64) for b in range(RP)]
        q_w = [keep.tile([P, NQ, PACK], BF16, name="q_w%d" % b, align_bytes=64) for b in range(RP)]
        page_q, x_q, q_q = {}, {}, {}

        nc.vector.tensor_copy(
            out=q_w[0][:].rearrange("p (c k) i -> p c i k", k=4), in_=q_raw[0][:].rearrange("p i (c k) -> p c i k", k=4)
        )
        q_q[0] = quantise(q_w[0][:], "q0")

        def put(b, i):
            for blocks in FIRST_PIECES if (b, i) == (0, 0) else [[0, 1, 2, 3]]:
                cols = slice(P * blocks[0], P * (blocks[-1] + 1))
                window = page[b, i][:].indirect(place[:, cols.start // 16 : cols.stop // 16])
                nc.vector.tensor_tensor(out=window, in0=feats[b, i][:, cols], in1=wg_dealt[i][:, cols], op=ALU.mult)
            if i < copied[b]:
                nc.sync.dma_start(out=page_side[b][:, i, :], in_=page[b, i][:])

        for b, i in order:
            rows = page[b, i]
            if i == 0:
                put(b, i)
                put(b, i + 1)
                picked = keep.tile([P, NQ], F32, name="picked", tag="held%d%d" % (b, i + 1), align_bytes=64)
            else:
                if i >= 2:
                    put(b, i)
                picked = small.tile([P, NQ], F32, name="picked", bufs=8)
            nc.vector.tensor_copy(out=picked[:], in_=rows[:].indirect(alarm[:]))
            scale = vec_t[:, b, i : i + 1]
            if b == 1 and i < 3:
                size = overlay.tile([P, NQ], F32, name="size%d" % i, offset=4 * T2 + 4 * NQ * (i % 2))
            else:
                size = small.tile([P, NQ], F32, name="size", bufs=2)
            if i < copied[b]:
                nc.scalar.activation(out=size[:], in_=picked[:], func=ACT.Abs)
                nc.scalar.activation(out=x_side[b][:, i, :], in_=size[:], func=ACT.Copy, scale=scale)
                if i == copied[b] - 1:
                    join = weave if b == 0 else weave_pair
                    join(x_w[b][:, :, 0 : i + 1], x_side[b][:])
                    for h in range(2 - b):
                        join(page_w[b, h][:, :, 0 : i + 1], page_side[b][:, :, HALF * h : HALF * (h + 1)])
                    if b == 0:
                        page[1, 3] = load_page(1, 3)
            else:
                nc.scalar.copy(out=page_w[b, 0][:, :, i], in_=rows[:, 0:HALF])
                nc.scalar.activation(out=size[:], in_=picked[:], func=ACT.Abs)
                if i == 2:
                    weave_pair(page_w[b, 1][:, :, 0:2], page_side[b][:, :, HALF:T2])
                else:
                    for r in (2, 3):
                        nc.scalar.copy(out=page_w[b, 1][:, :, r], in_=page[b, r][:, HALF:T2])
                nc.vector.tensor_scalar(
                    out=x_w[b][:, :, i], in0=size[:], scalar1=scale, scalar2=None, op0=ALU.mult
                )
            if (b, i) == (0, 1):
                weave(q_w[1][:], q_raw[1][:])
            if (b, i) == (1, 2):
                planes = keep.tile([P, 2, HALF], U8, name="planes", tag="held12", align_bytes=64)
                page_q[0, 0] = quantise(page_w[0, 0][:], "page00", planes[:, 0, :])
                x_q[0] = quantise(x_w[0][:], "x0", planes[:, 1, :])
        planes = keep.tile([P, 2, HALF], U8, name="late_planes", tag="held13", align_bytes=64)
        q_q[1] = quantise(q_w[1][:], "q1", planes[:, 0, :])
        page_q[1, 0] = quantise(page_w[1, 0][:], "page10")
        page_q[0, 1] = quantise(page_w[0, 1][:], "page01", planes[:, 1, :])
        x_q[1] = quantise(x_w[1][:], "x1")
        page_q[1, 1] = quantise(page_w[1, 1][:], "page11")

        def scores(mt, moving):
            acc = psum.tile([P, NQ], F32, name="acc", tag="bank")
            h, cols = mt // 4, slice(P * (mt % 4), P * (mt % 4 + 1))
            for b in range(RP):
                nc.tensor.matmul_mx(
                    out=acc[:],
                    lhsT=page_q[b, h][0][:, cols].bitcast(FP8X4),
                    lhsT_scale=page_q[b, h][1][:, cols],
                    rhs=moving[b][0].bitcast(FP8X4),
                    rhs_scale=moving[b][1],
                    start=(b == 0),
                    stop=(b == RP - 1),
                )
            return acc

        def query_scores(mt):
            f = scores(mt, q_q)
            f_sb = ring.tile([P, NQ], F32, name="f_sb", tag="ring_a")
            nc.scalar.copy(out=f_sb[:], in_=f[:])
            return f_sb

        def finish(mt, f_sb):
            e = scores(mt, x_q)
            larger = small.tile([P, NQ], F32, name="larger", tag="picked", bufs=8)
            nc.vector.tensor_tensor(out=larger[:], in0=e[:], in1=f_sb[:], op=ALU.max)
            result = ring.tile([P, NQ], F32, name="result", tag="ring_b", bufs=7)
            adder = nc.gpsimd if mt < ADDS_ON_GPSIMD else nc.vector
            adder.tensor_tensor(out=result[:], in0=larger[:], in1=base_t[mt // 4][:, mt % 4, :], op=ALU.add)
            nc.sync.dma_start(out=out[P * mt : P * (mt + 1), :], in_=result[:])

        first_half = [query_scores(mt) for mt in range(4)]
        for mt in range(4):
            finish(mt, first_half[mt])
        for mt in range(4, T2 // P):
            finish(mt, query_scores(mt))
